import numpy as np
import ml_dtypes


def mxq(x, axis, fmt="e4m3"):
    dtype, down = {"e4m3": (ml_dtypes.float8_e4m3fn, 7), "e5m2": (ml_dtypes.float8_e5m2, 14)}[fmt]
    v = np.moveaxis(np.asarray(x, np.float32).astype(ml_dtypes.bfloat16).astype(np.float64), axis, -1)
    blocks = v.reshape(v.shape[:-1] + (-1, 32))
    amax = np.abs(blocks).max(-1, keepdims=True)
    byte = np.maximum(np.where(amax > 0, np.frexp(amax)[1] - 1 + 127, 0) - down, 1)
    scale = np.exp2(byte - 127.0)
    codes = (blocks / scale).astype(np.float32).astype(dtype).astype(np.float64)
    return np.moveaxis((codes * scale).reshape(v.shape), -1, axis)


WIDE = False


def mx_kscale(k):
    if not WIDE:
        return np.ones(k)
    levels = np.array([10, -10, 5, -5, 0])
    if k % 512:
        return np.exp2(np.random.permutation(np.resize(levels, k // 32))).repeat(32)
    a = np.empty((k // 512, 16))
    for p in range(k // 512):
        a[p, :8] = np.random.permutation(np.resize(levels, 8))
        for g in range(8):
            far = levels[np.abs(levels - a[p, g]) >= 10]
            a[p, g + 8] = far[np.random.randint(len(far))]
    return np.exp2(a.ravel()).repeat(32)


def f64(x):
    return np.asarray(x).astype(np.float64)


def striped(idx):
    return np.tile(np.asarray(idx).reshape(-1, 16).T, (8, 1)).astype(np.uint16)


def unstriped(offs):
    return offs[:16].T.reshape(-1).astype(np.int64)


def striped8(idx):
    return np.asarray(idx).reshape(8, -1, 16).transpose(0, 2, 1).reshape(128, -1).astype(np.uint16)


def unstriped8(offs):
    return offs.reshape(8, 16, -1).transpose(0, 2, 1).reshape(8, -1).astype(np.int64)


def pick8(x, idx, run):
    r = np.arange(len(x))
    return x[r[:, None], idx[r % (8 * run) // run]]


E2M1 = np.array([0.0, 0.5, 1.0, 1.5, 2.0, 3.0, 4.0, 6.0, -0.0, -0.5, -1.0, -1.5, -2.0, -3.0, -4.0, -6.0])


def pack_weight(w, fmt):
    k, n = w.shape
    w = f64(np.asarray(w, np.float32).astype(ml_dtypes.bfloat16)).reshape(k // 32, 32, n)
    amax = np.abs(w).max(1)
    if fmt == "e4m3":
        byte = np.frexp(amax)[1] - 1 + 127 - 7
    else:
        mant, ex = np.frexp(amax / 6.0)
        byte = np.where(mant > 0.5, ex, ex - 1) + 127
    byte = np.clip(np.where(amax > 0, byte, 1), 1, 254)
    scaled = (w * np.exp2(127.0 - byte)[:, None, :]).reshape(k, n).astype(np.float32)
    by_word = np.ascontiguousarray(scaled.reshape(k // 512, 128, 4, n).transpose(0, 1, 3, 2))
    if fmt == "e4m3":
        words = by_word.astype(ml_dtypes.float8_e4m3fn).view(np.uint8)
    else:
        c = by_word.astype(ml_dtypes.float4_e2m1fn).view(np.uint8) & 0xF
        words = (c[..., 0::2] | (c[..., 1::2] << 4)).reshape(k // 512, 128, 2 * n)
    return np.ascontiguousarray(words), np.ascontiguousarray(byte.astype(np.uint8).reshape(k // 512, 16, n))


def unpack_weight(words, scales, fmt):
    g, _, n = scales.shape
    words = np.ascontiguousarray(words).reshape(g, 128, n, -1)
    if fmt == "e4m3":
        vals = words.view(ml_dtypes.float8_e4m3fn).astype(np.float64)
    else:
        nib = np.empty((g, 128, n, 4), np.uint8)
        nib[..., 0::2] = words & 0xF
        nib[..., 1::2] = words >> 4
        vals = E2M1[nib]
    vals = vals * np.repeat(np.exp2(scales.astype(np.float64) - 127.0), 8, axis=1)[..., None]
    return vals.transpose(0, 1, 3, 2).reshape(g * 512, n)


K, J, R, T, O, S, N, Z, V, U = 512, 1024, 512, 2048, 256, 512, 256, 512, 1024, 128


def setup_inputs():
    n = np.random.standard_normal
    idx = np.stack([np.random.permutation(T)[:J] for _ in range(8)])
    idx2 = np.stack([np.random.permutation(J)[:S] for _ in range(8)])
    idx3 = np.stack([np.random.permutation(S)[:O] for _ in range(8)])
    idx4 = np.random.permutation(S)[:O]
    idx5 = np.random.permutation(V)[:O]
    idx6 = np.stack([np.random.permutation(O)[:U] for _ in range(8)])
    idx7 = np.stack([np.random.permutation(O)[:U] for _ in range(8)])
    fk = mx_kscale(K)
    fr = mx_kscale(R)
    fz = mx_kscale(Z)
    wp = pack_weight(n((K, R)) * 1 / np.sqrt(K) / fk[:, None] * fr, "e2m1")
    wbp = pack_weight(n((R, N)) * 1 / np.sqrt(R) / fr[:, None], "e4m3")
    xrp = pack_weight(n((Z, V)) / fz[:, None], "e2m1")
    wsp = pack_weight(n((Z, N)) * 1 / np.sqrt(Z) * fz[:, None], "e4m3")
    return {
        "ta": (np.random.randint(-7, 8, (K, T)).astype(np.float64)).astype(np.float32),
        "ga": ((np.random.randint(8, 25, (K, 1)) / 64.0) * fk[:, None]).astype(np.float32),
        "w_words": wp[0],
        "w_scales": wp[1],
        "sa": (np.random.uniform(0.5, 1.6, (R, 1))).astype(np.float32),
        "sb": (np.random.uniform(0.5, 1.6, (R, 1))).astype(np.float32),
        "sd": (np.random.uniform(0.5, 1.6, (R, 1))).astype(np.float32),
        "wb_words": wbp[0],
        "wb_scales": wbp[1],
        "xr_words": xrp[0],
        "xr_scales": xrp[1],
        "ws_words": wsp[0],
        "ws_scales": wsp[1],
        "so": (np.random.uniform(0.5, 1.6, (N, 1))).astype(np.float32),
        "sp": (np.random.uniform(0.5, 1.6, (N, 1))).astype(np.float32),
        "offs": striped8(idx),
        "offs2": striped8(idx2),
        "offs3": striped8(idx3),
        "offs4": striped(idx4),
        "offs5": striped(idx5),
        "offs6": striped8(idx6),
        "offs7": striped8(idx7),
    }


def reference(ta, ga, w_words, w_scales, sa, sb, sd, wb_words, wb_scales, xr_words, xr_scales, ws_words, ws_scales, so, sp, offs, offs2, offs3, offs4, offs5, offs6, offs7):
    idx = unstriped8(offs)
    idx2 = unstriped8(offs2)
    idx3 = unstriped8(offs3)
    idx4 = unstriped(offs4)
    idx5 = unstriped(offs5)
    idx6 = unstriped8(offs6)
    idx7 = unstriped8(offs7)
    wu = unpack_weight(w_words, w_scales, "e2m1")
    wbu = unpack_weight(wb_words, wb_scales, "e4m3")
    xru = unpack_weight(xr_words, xr_scales, "e2m1")
    wsu = unpack_weight(ws_words, ws_scales, "e4m3")
    xc = pick8(f64(ta), idx, 64) * f64(ga)
    xcq = mxq(xc, 0, "e4m3")
    a = wu.T @ xcq
    h1 = pick8(a, idx2, 64) * f64(sa)
    hid = np.abs(pick8(h1, idx3, 64) * f64(sb) - h1[:, idx4] * f64(sd))
    hidq = mxq(hid, 0, "e4m3")
    xridx5g = xru[:, idx5]
    p = wbu.T @ hidq + wsu.T @ xridx5g
    y = np.maximum(pick8(p, idx6, 16) * f64(so), pick8(p, idx7, 16) * f64(sp))
    return y

@@ -1,0 +1,227 @@
+from contextlib import ExitStack
+
+import concourse.mybir as mybir
+
+K, J, R, T, O, S, N, Z, V, U = 512, 1024, 512, 2048, 256, 512, 256, 512, 1024, 128
+FLOPS = 2 * (K * R * J + R * N * O + Z * N * O)
+
+F32 = mybir.dt.float32
+BF16 = mybir.dt.bfloat16
+I32 = mybir.dt.int32
+U32 = mybir.dt.uint32
+U16 = mybir.dt.uint16
+U8 = mybir.dt.uint8
+FP8X4 = mybir.dt.float8_e4m3fn_x4
+FP4X4 = mybir.dt.float4_e2m1fn_x4
+ACT = mybir.ActivationFunctionType
+ALU = mybir.AluOpType
+
+P = 128
+PACK = 4
+STRIPE = 16
+ALIGN = 64
+HJ = J // 2
+QJ = J // 4
+HO = O // 2
+
+
+def tile_picked_codes_plain_one_chain_reminder_grouppairs_kernel(
+    tc, ta, ga, w_words, w_scales, sa, sb, sd, wb_words, wb_scales, xr_words, xr_scales,
+    ws_words, ws_scales, so, sp, offs, offs2, offs3, offs4, offs5, offs6, offs7, out,
+):
+    nc = tc.nc
+
+    with ExitStack() as ctx:
+        lists = ctx.enter_context(tc.tile_pool(name="lists", bufs=1))
+        keep = ctx.enter_context(tc.tile_pool(name="keep", bufs=1))
+        psum = ctx.enter_context(tc.psum_pool(name="psum", bufs=1))
+
+        def load_list(name, source):
+            tile = lists.tile(list(source.shape), U16, name=name)
+            nc.sync.dma_start(tile[:], source)
+            return tile
+
+        def load_dealt(name, source, queue):
+            tile = keep.tile([P, PACK], F32, name=name)
+            queue.dma_start(tile[:], source.rearrange("(p t) one -> p (t one)", t=PACK))
+            return tile
+
+        def load_blocks(name, source):
+            tile = keep.tile([P, N // P], F32, name=name)
+            with nc.allow_non_contiguous_dma(reason="one value a partition"):
+                nc.sync.dma_start(tile[:], source.rearrange("(u p) one -> p (u one)", p=P))
+            return tile
+
+        def zeroed_plane(name, width):
+            plane = keep.tile([P, width], U8, name=name, align_bytes=ALIGN)
+            nc.vector.memset(plane[:].bitcast(I32), 0)
+            return plane
+
+        def load_scale_rows(plane, source):
+            for q in range(4):
+                nc.sync.dma_start(plane[32 * q:32 * q + 4, :].bitcast(I32), source[0, 4 * q:4 * q + 4, :].bitcast(I32))
+
+        def load_e4m3_words(name, source):
+            tile = keep.tile([P, N], U32, name=name, align_bytes=ALIGN)
+            nc.sync.dma_start(tile[:].bitcast(I32), source[0].rearrange("p n t -> p (n t)").bitcast(I32))
+            return tile
+
+        def fetch(dst, window, lst, first, count, scale):
+            nc.scalar.activation(
+                out=dst, in_=window[:].indirect(lst[:, first // STRIPE:(first + count) // STRIPE]),
+                func=ACT.Copy, scale=scale,
+            )
+
+        l1 = load_list("l1", offs)
+        ga_t = load_dealt("ga_t", ga, nc.scalar)
+        ta_rows = ta.rearrange("(p t) c -> t p c", t=PACK)
+        ta_t = [keep.tile([P, T], F32, name="ta%d" % t) for t in range(PACK)]
+        nc.sync.dma_start(ta_t[0][:], ta_rows[0])
+        nc.sync.dma_start(ta_t[1][:], ta_rows[1])
+        w_raw = keep.tile([P, 2 * R], U8, name="w_raw")
+        nc.sync.dma_start(w_raw[:].bitcast(I32), w_words[0].bitcast(I32))
+        w_stage = keep.tile([4, 4, R], U8, name="w_stage")
+        nc.sync.dma_start(w_stage[:].bitcast(I32), w_scales[0].rearrange("(q r) n -> r q n", r=4).bitcast(I32))
+        nc.sync.dma_start(ta_t[2][:], ta_rows[2])
+        nc.sync.dma_start(ta_t[3][:], ta_rows[3])
+
+        w_plane = zeroed_plane("w_plane", R)
+        xr_plane = zeroed_plane("xr_plane", V)
+        ws_plane = zeroed_plane("ws_plane", N)
+        wb_plane = zeroed_plane("wb_plane", N)
+
+        l2 = load_list("l2", offs2)
+        sa_t = load_dealt("sa_t", sa, nc.sync)
+        l3 = load_list("l3", offs3)
+        l4 = load_list("l4", offs4)
+        sb_t = load_dealt("sb_t", sb, nc.sync)
+        sd_t = load_dealt("sd_t", sd, nc.sync)
+        l5 = load_list("l5", offs5)
+        xr_win = keep.tile([P, V], U16, name="xr_win")
+        nc.sync.dma_start(xr_win[:].bitcast(I32), xr_words[0].bitcast(I32))
+        load_scale_rows(xr_plane, xr_scales)
+        ws_w = load_e4m3_words("ws_w", ws_words)
+        load_scale_rows(ws_plane, ws_scales)
+        wb_w = load_e4m3_words("wb_w", wb_words)
+        load_scale_rows(wb_plane, wb_scales)
+        l6 = load_list("l6", offs6)
+        l7 = load_list("l7", offs7)
+        so_t = load_blocks("so_t", so)
+        sp_t = load_blocks("sp_t", sp)
+
+        for q in range(4):
+            nc.vector.tensor_copy(w_plane[32 * q:32 * q + 4, :].bitcast(I32), w_stage[:, q, :].bitcast(I32))
+        w_dw = keep.tile([P, PACK, 2 * P], U8, name="w_dw", tag="fp4_words", align_bytes=ALIGN)
+        w_ds = keep.tile([P, PACK, P], U8, name="w_ds", tag="fp4_scales", align_bytes=ALIGN)
+        nc.vector.tensor_copy(
+            w_dw[:].rearrange("p t (m b) -> p t m b", b=2),
+            w_raw[:].rearrange("p (m t b) -> p t m b", t=PACK, b=2),
+        )
+        nc.vector.tensor_copy(w_ds[:], w_plane[:].rearrange("p (m t) -> p t m", t=PACK))
+
+        chunks = [(0, HJ), (HJ, QJ), (HJ + QJ, QJ)]
+        xc4 = [keep.tile([P, n, PACK], BF16, name="xc4_%d" % c, align_bytes=ALIGN) for c, (j0, n) in enumerate(chunks)]
+        g01 = keep.tile([P, 2, J], BF16, name="g01")
+        g23 = [keep.tile([P, 2, HJ], BF16, name="g23_%d" % h) for h in range(2)]
+        for t in range(2):
+            fetch(g01[:, t, :], ta_t[t], l1, 0, J, ga_t[:, t:t + 1])
+        for c, (j0, n) in enumerate(chunks):
+            nc.vector.tensor_copy(xc4[c][:, :, 0:2], g01[:, :, j0:j0 + n].rearrange("p e j -> p j e"))
+        for t in range(2, PACK):
+            for h in range(2):
+                fetch(g23[h][:, t - 2, :], ta_t[t], l1, h * HJ, HJ, ga_t[:, t:t + 1])
+
+        xq = [keep.tile([P, HJ], U32, name="xq%d" % h, align_bytes=ALIGN) for h in range(2)]
+        xs = [keep.tile([P, HJ], U8, name="xs%d" % h, align_bytes=ALIGN) for h in range(2)]
+        for c, (j0, n) in enumerate(chunks):
+            h, c0 = divmod(j0, HJ)
+            src = g23[h][:, :, c0:c0 + n].rearrange("p e j -> p j e")
+            if c == len(chunks) - 1:
+                nc.scalar.copy(xc4[c][:, :, 2:4], src)
+            else:
+                nc.vector.tensor_copy(xc4[c][:, :, 2:4], src)
+            nc.vector.quantize_mx(
+                out=xq[h][:, c0:c0 + n].bitcast(FP8X4), scales=xs[h][:, c0:c0 + n],
+                in_=xc4[c][:].rearrange("p j t -> p (j t)"),
+            )
+
+        a_t = [keep.tile([P, J], F32, name="a%d" % t) for t in range(PACK)]
+        pieces = [(0, j0, n, c) for c, (j0, n) in enumerate(chunks)]
+        for t in range(1, PACK):
+            pieces.extend([(t, 0, HJ, t - 1), (t, HJ, HJ, 2 + t)])
+        for t, j0, n, bank in pieces:
+            h, c0 = divmod(j0, HJ)
+            acc = psum.tile([P, n], F32, name="acc", tag="bank%d" % bank)
+            nc.tensor.matmul_mx(
+                out=acc[:], lhsT=w_dw[:, t, :].bitcast(FP4X4), lhsT_scale=w_ds[:, t, :],
+                rhs=xq[h][:, c0:c0 + n].bitcast(FP8X4), rhs_scale=xs[h][:, c0:c0 + n], start=True, stop=True,
+            )
+            if (t, j0) == (0, 0):
+                nc.scalar.copy(a_t[t][:, j0:j0 + n], acc[:])
+            else:
+                nc.vector.tensor_copy(a_t[t][:, j0:j0 + n], acc[:])
+
+        xr_gw = keep.tile([P, O], U16, name="xr_gw", tag="fp4_words", align_bytes=ALIGN)
+        xr_gs = keep.tile([P, O], U8, name="xr_gs", tag="fp4_scales", align_bytes=ALIGN)
+        nc.vector.tensor_copy(xr_gw[:], xr_win[:].indirect(l5[:]))
+        nc.vector.tensor_copy(xr_gs[:], xr_plane[:].indirect(l5[:]))
+        p_banks = [[6, 7], [3, 4]]
+        pacc = [[psum.tile([P, HO], F32, name="pacc", tag="bank%d" % p_banks[h][u]) for u in range(2)] for h in range(2)]
+        for h in range(2):
+            for u in range(2):
+                nc.tensor.matmul_mx(
+                    out=pacc[h][u][:], lhsT=ws_w[:, u * P:(u + 1) * P].bitcast(FP8X4), lhsT_scale=ws_plane[:, u * P:(u + 1) * P],
+                    rhs=xr_gw[:, h * HO:(h + 1) * HO].bitcast(FP4X4), rhs_scale=xr_gs[:, h * HO:(h + 1) * HO],
+                    start=True, stop=False,
+                )
+
+        hid4 = [keep.tile([P, HO, PACK], BF16, name="hid4_%d" % h, align_bytes=ALIGN) for h in range(2)]
+        d01 = keep.tile([P, 2, O], BF16, name="d01")
+        d23 = [keep.tile([P, 2, HO], BF16, name="d23_%d" % h) for h in range(2)]
+
+        def magnitude(dst, src):
+            view = src.rearrange("p e o -> p o e")
+            nc.vector.scalar_tensor_tensor(dst, view, -1.0, view, ALU.mult, ALU.max)
+
+        p_t = [keep.tile([P, O], F32, name="p%d" % u) for u in range(2)]
+        for t in range(PACK):
+            h1 = keep.tile([P, S], F32, name="h1_%d" % t)
+            fetch(h1[:], a_t[t], l2, 0, S, sa_t[:, t:t + 1])
+            spans = [(0, O)] if t < PACK - 1 else [(0, HO), (HO, HO)]
+            for o0, n in spans:
+                own = keep.tile([P, n], F32, name="own_%d_%d" % (t, o0))
+                shared = keep.tile([P, n], F32, name="shared_%d_%d" % (t, o0))
+                fetch(own[:], h1, l3, o0, n, sb_t[:, t:t + 1])
+                fetch(shared[:], h1, l4, o0, n, sd_t[:, t:t + 1])
+                if t < 2:
+                    nc.vector.tensor_tensor(d01[:, t, :], own[:], shared[:], ALU.subtract)
+                else:
+                    for h in range(o0 // HO, (o0 + n) // HO):
+                        cols = slice(h * HO - o0, (h + 1) * HO - o0)
+                        nc.vector.tensor_tensor(d23[h][:, t - 2, :], own[:, cols], shared[:, cols], ALU.subtract)
+                if t == 1:
+                    for h in range(2):
+                        magnitude(hid4[h][:, :, 0:2], d01[:, :, h * HO:(h + 1) * HO])
+                if t == PACK - 1:
+                    h = o0 // HO
+                    magnitude(hid4[h][:, :, 2:4], d23[h][:])
+                    hq = keep.tile([P, HO], U32, name="hq%d" % h, align_bytes=ALIGN)
+                    hs = keep.tile([P, HO], U8, name="hs%d" % h, align_bytes=ALIGN)
+                    nc.vector.quantize_mx(out=hq[:].bitcast(FP8X4), scales=hs[:], in_=hid4[h][:].rearrange("p o t -> p (o t)"))
+                    for u in range(2):
+                        nc.tensor.matmul_mx(
+                            out=pacc[h][u][:], lhsT=wb_w[:, u * P:(u + 1) * P].bitcast(FP8X4), lhsT_scale=wb_plane[:, u * P:(u + 1) * P],
+                            rhs=hq[:].bitcast(FP8X4), rhs_scale=hs[:], start=False, stop=True,
+                        )
+        for h in range(2):
+            nc.scalar.copy(p_t[0][:, h * HO:(h + 1) * HO], pacc[h][0][:])
+            nc.vector.tensor_copy(p_t[1][:, h * HO:(h + 1) * HO], pacc[h][1][:])
+
+        for u in range(2):
+            first = keep.tile([P, U], F32, name="first%d" % u)
+            second = keep.tile([P, U], F32, name="second%d" % u)
+            larger = keep.tile([P, U], F32, name="larger%d" % u)
+            fetch(first[:], p_t[u], l6, 0, U, so_t[:, u:u + 1])
+            fetch(second[:], p_t[u], l7, 0, U, sp_t[:, u:u + 1])
+            nc.vector.tensor_tensor(larger[:], first[:], second[:], ALU.max)
+            nc.sync.dma_start(out[u * P:(u + 1) * P, :], larger[:])

@@ -72,6 +72,11 @@ def tile_picked_codes_plain_one_chain_reminder_grouppairs_kernel(
                 func=ACT.Copy, scale=scale,
             )
 
+        warm_in = keep.tile([P, 1], F32, name="warm_in")
+        warm_out = keep.tile([P, 1], F32, name="warm_out")
+        nc.gpsimd.memset(warm_in[:], 0.0)
+        nc.scalar.activation(out=warm_out[:], in_=warm_in[:], func=ACT.Copy)
+
         l1 = load_list("l1", offs)
         ga_t = load_dealt("ga_t", ga, nc.scalar)
         ta_rows = ta.rearrange("(p t) c -> t p c", t=PACK)

@@ -77,11 +77,11 @@ def tile_picked_codes_plain_one_chain_reminder_grouppairs_kernel(
         nc.gpsimd.memset(warm_in[:], 0.0)
         nc.scalar.activation(out=warm_out[:], in_=warm_in[:], func=ACT.Copy)
 
-        l1 = load_list("l1", offs)
         ga_t = load_dealt("ga_t", ga, nc.scalar)
         ta_rows = ta.rearrange("(p t) c -> t p c", t=PACK)
         ta_t = [keep.tile([P, T], F32, name="ta%d" % t) for t in range(PACK)]
         nc.sync.dma_start(ta_t[0][:], ta_rows[0])
+        l1 = load_list("l1", offs)
         nc.sync.dma_start(ta_t[1][:], ta_rows[1])
         w_raw = keep.tile([P, 2 * R], U8, name="w_raw")
         nc.sync.dma_start(w_raw[:].bitcast(I32), w_words[0].bitcast(I32))
@@ -95,16 +95,16 @@ def tile_picked_codes_plain_one_chain_reminder_grouppairs_kernel(
         ws_plane = zeroed_plane("ws_plane", N)
         wb_plane = zeroed_plane("wb_plane", N)
 
-        l2 = load_list("l2", offs2)
-        sa_t = load_dealt("sa_t", sa, nc.sync)
-        l3 = load_list("l3", offs3)
-        l4 = load_list("l4", offs4)
-        sb_t = load_dealt("sb_t", sb, nc.sync)
-        sd_t = load_dealt("sd_t", sd, nc.sync)
         l5 = load_list("l5", offs5)
         xr_win = keep.tile([P, V], U16, name="xr_win")
         nc.sync.dma_start(xr_win[:].bitcast(I32), xr_words[0].bitcast(I32))
         load_scale_rows(xr_plane, xr_scales)
+        l3 = load_list("l3", offs3)
+        l4 = load_list("l4", offs4)
+        sb_t = load_dealt("sb_t", sb, nc.sync)
+        sd_t = load_dealt("sd_t", sd, nc.sync)
+        l2 = load_list("l2", offs2)
+        sa_t = load_dealt("sa_t", sa, nc.sync)
         ws_w = load_e4m3_words("ws_w", ws_words)
         load_scale_rows(ws_plane, ws_scales)
         wb_w = load_e4m3_words("wb_w", wb_words)
@@ -124,44 +124,50 @@ def tile_picked_codes_plain_one_chain_reminder_grouppairs_kernel(
         )
         nc.vector.tensor_copy(w_ds[:], w_plane[:].rearrange("p (m t) -> p t m", t=PACK))
 
-        chunks = [(0, HJ), (HJ, QJ), (HJ + QJ, QJ)]
+        EJ = J // 8
+        chunks = [(0, QJ), (QJ, QJ), (HJ, QJ), (HJ + QJ, EJ), (HJ + QJ + EJ, EJ)]
+        on_scalar = [3, 4]
         xc4 = [keep.tile([P, n, PACK], BF16, name="xc4_%d" % c, align_bytes=ALIGN) for c, (j0, n) in enumerate(chunks)]
         g01 = keep.tile([P, 2, J], BF16, name="g01")
-        g23 = [keep.tile([P, 2, HJ], BF16, name="g23_%d" % h) for h in range(2)]
         for t in range(2):
             fetch(g01[:, t, :], ta_t[t], l1, 0, J, ga_t[:, t:t + 1])
         for c, (j0, n) in enumerate(chunks):
             nc.vector.tensor_copy(xc4[c][:, :, 0:2], g01[:, :, j0:j0 + n].rearrange("p e j -> p j e"))
-        for t in range(2, PACK):
-            for h in range(2):
-                fetch(g23[h][:, t - 2, :], ta_t[t], l1, h * HJ, HJ, ga_t[:, t:t + 1])
-
         xq = [keep.tile([P, HJ], U32, name="xq%d" % h, align_bytes=ALIGN) for h in range(2)]
         xs = [keep.tile([P, HJ], U8, name="xs%d" % h, align_bytes=ALIGN) for h in range(2)]
-        for c, (j0, n) in enumerate(chunks):
-            h, c0 = divmod(j0, HJ)
-            src = g23[h][:, :, c0:c0 + n].rearrange("p e j -> p j e")
-            if c == len(chunks) - 1:
-                nc.scalar.copy(xc4[c][:, :, 2:4], src)
-            else:
-                nc.vector.tensor_copy(xc4[c][:, :, 2:4], src)
-            nc.vector.quantize_mx(
-                out=xq[h][:, c0:c0 + n].bitcast(FP8X4), scales=xs[h][:, c0:c0 + n],
-                in_=xc4[c][:].rearrange("p j t -> p (j t)"),
-            )
+        quantise_order = [[0, 1], [3, 2, 4]]
+        for t in range(2, PACK):
+            for h in range(2):
+                tag = "g_upper" if h == 1 else "g_lower%d" % t
+                g = keep.tile([P, HJ], BF16, name="g", tag=tag)
+                fetch(g[:], ta_t[t], l1, h * HJ, HJ, ga_t[:, t:t + 1])
+                for c, (j0, n) in enumerate(chunks):
+                    if j0 // HJ == h:
+                        src = g[:, j0 - h * HJ:j0 - h * HJ + n]
+                        if t == PACK - 1 and c in on_scalar:
+                            nc.scalar.copy(xc4[c][:, :, t], src)
+                        else:
+                            nc.vector.tensor_copy(xc4[c][:, :, t], src)
+                if t == PACK - 1:
+                    for c in quantise_order[h]:
+                        j0, n = chunks[c]
+                        c0 = j0 - h * HJ
+                        nc.vector.quantize_mx(
+                            out=xq[h][:, c0:c0 + n].bitcast(FP8X4), scales=xs[h][:, c0:c0 + n],
+                            in_=xc4[c][:].rearrange("p j t -> p (j t)"),
+                        )
 
         a_t = [keep.tile([P, J], F32, name="a%d" % t) for t in range(PACK)]
-        pieces = [(0, j0, n, c) for c, (j0, n) in enumerate(chunks)]
-        for t in range(1, PACK):
-            pieces.extend([(t, 0, HJ, t - 1), (t, HJ, HJ, 2 + t)])
-        for t, j0, n, bank in pieces:
+        pieces = [(0, 0, HJ, 0), (1, 0, HJ, 4), (0,) + chunks[3] + (1,), (0,) + chunks[2] + (2,), (0,) + chunks[4] + (3,),
+                  (1, HJ, HJ, 5), (2, HJ, HJ, 6), (2, 0, HJ, 3), (3, HJ, HJ, 7), (3, 0, HJ, 2)]
+        for i, (t, j0, n, bank) in enumerate(pieces):
             h, c0 = divmod(j0, HJ)
             acc = psum.tile([P, n], F32, name="acc", tag="bank%d" % bank)
             nc.tensor.matmul_mx(
                 out=acc[:], lhsT=w_dw[:, t, :].bitcast(FP4X4), lhsT_scale=w_ds[:, t, :],
                 rhs=xq[h][:, c0:c0 + n].bitcast(FP8X4), rhs_scale=xs[h][:, c0:c0 + n], start=True, stop=True,
             )
-            if (t, j0) == (0, 0):
+            if i in (0, 1, 4):
                 nc.scalar.copy(a_t[t][:, j0:j0 + n], acc[:])
             else:
                 nc.vector.tensor_copy(a_t[t][:, j0:j0 + n], acc[:])
@@ -170,7 +176,7 @@ def tile_picked_codes_plain_one_chain_reminder_grouppairs_kernel(
         xr_gs = keep.tile([P, O], U8, name="xr_gs", tag="fp4_scales", align_bytes=ALIGN)
         nc.vector.tensor_copy(xr_gw[:], xr_win[:].indirect(l5[:]))
         nc.vector.tensor_copy(xr_gs[:], xr_plane[:].indirect(l5[:]))
-        p_banks = [[6, 7], [3, 4]]
+        p_banks = [[0, 1], [4, 5]]
         pacc = [[psum.tile([P, HO], F32, name="pacc", tag="bank%d" % p_banks[h][u]) for u in range(2)] for h in range(2)]
         for h in range(2):
             for u in range(2):
@@ -188,36 +194,48 @@ def tile_picked_codes_plain_one_chain_reminder_grouppairs_kernel(
             view = src.rearrange("p e o -> p o e")
             nc.vector.scalar_tensor_tensor(dst, view, -1.0, view, ALU.mult, ALU.max)
 
+        h1 = [keep.tile([P, S], F32, name="h1_%d" % t) for t in range(PACK)]
+
+        def seats(t):
+            fetch(h1[t][:], a_t[t], l2, 0, S, sa_t[:, t:t + 1])
+
+        def difference(t, o0, n):
+            own = keep.tile([P, n], F32, name="own_%d_%d" % (t, o0))
+            shared = keep.tile([P, n], F32, name="shared_%d_%d" % (t, o0))
+            fetch(own[:], h1[t], l3, o0, n, sb_t[:, t:t + 1])
+            fetch(shared[:], h1[t], l4, o0, n, sd_t[:, t:t + 1])
+            if t < 2:
+                nc.vector.tensor_tensor(d01[:, t, :], own[:], shared[:], ALU.subtract)
+            else:
+                for h in range(o0 // HO, (o0 + n) // HO):
+                    cols = slice(h * HO - o0, (h + 1) * HO - o0)
+                    nc.vector.tensor_tensor(d23[h][:, t - 2, :], own[:, cols], shared[:, cols], ALU.subtract)
+            return shared
+
+        seats(0)
+        for t in range(PACK - 1):
+            seats(t + 1)
+            difference(t, 0, O)
+            if t == 1:
+                for h in range(2):
+                    magnitude(hid4[h][:, :, 0:2], d01[:, :, h * HO:(h + 1) * HO])
+        for h in range(2):
+            last = difference(PACK - 1, h * HO, HO)
+        QO = HO // 2
+        nc.scalar.activation(out=hid4[0][:, :, 2:4], in_=d23[0][:].rearrange("p e o -> p o e"), func=ACT.Abs)
+        magnitude(hid4[1][:, :QO, 2:4], d23[1][:, :, :QO])
+        nc.scalar.activation(out=hid4[1][:, QO:, 2:4], in_=d23[1][:, :, QO:].rearrange("p e o -> p o e"), func=ACT.Abs)
+
         p_t = [keep.tile([P, O], F32, name="p%d" % u) for u in range(2)]
-        for t in range(PACK):
-            h1 = keep.tile([P, S], F32, name="h1_%d" % t)
-            fetch(h1[:], a_t[t], l2, 0, S, sa_t[:, t:t + 1])
-            spans = [(0, O)] if t < PACK - 1 else [(0, HO), (HO, HO)]
-            for o0, n in spans:
-                own = keep.tile([P, n], F32, name="own_%d_%d" % (t, o0))
-                shared = keep.tile([P, n], F32, name="shared_%d_%d" % (t, o0))
-                fetch(own[:], h1, l3, o0, n, sb_t[:, t:t + 1])
-                fetch(shared[:], h1, l4, o0, n, sd_t[:, t:t + 1])
-                if t < 2:
-                    nc.vector.tensor_tensor(d01[:, t, :], own[:], shared[:], ALU.subtract)
-                else:
-                    for h in range(o0 // HO, (o0 + n) // HO):
-                        cols = slice(h * HO - o0, (h + 1) * HO - o0)
-                        nc.vector.tensor_tensor(d23[h][:, t - 2, :], own[:, cols], shared[:, cols], ALU.subtract)
-                if t == 1:
-                    for h in range(2):
-                        magnitude(hid4[h][:, :, 0:2], d01[:, :, h * HO:(h + 1) * HO])
-                if t == PACK - 1:
-                    h = o0 // HO
-                    magnitude(hid4[h][:, :, 2:4], d23[h][:])
-                    hq = keep.tile([P, HO], U32, name="hq%d" % h, align_bytes=ALIGN)
-                    hs = keep.tile([P, HO], U8, name="hs%d" % h, align_bytes=ALIGN)
-                    nc.vector.quantize_mx(out=hq[:].bitcast(FP8X4), scales=hs[:], in_=hid4[h][:].rearrange("p o t -> p (o t)"))
-                    for u in range(2):
-                        nc.tensor.matmul_mx(
-                            out=pacc[h][u][:], lhsT=wb_w[:, u * P:(u + 1) * P].bitcast(FP8X4), lhsT_scale=wb_plane[:, u * P:(u + 1) * P],
-                            rhs=hq[:].bitcast(FP8X4), rhs_scale=hs[:], start=False, stop=True,
-                        )
+        for h in range(2):
+            hq = keep.tile([P, HO], U32, name="hq%d" % h, align_bytes=ALIGN)
+            hs = keep.tile([P, HO], U8, name="hs%d" % h, align_bytes=ALIGN)
+            nc.vector.quantize_mx(out=hq[:].bitcast(FP8X4), scales=hs[:], in_=hid4[h][:].rearrange("p o t -> p (o t)"))
+            for u in range(2):
+                nc.tensor.matmul_mx(
+                    out=pacc[h][u][:], lhsT=wb_w[:, u * P:(u + 1) * P].bitcast(FP8X4), lhsT_scale=wb_plane[:, u * P:(u + 1) * P],
+                    rhs=hq[:].bitcast(FP8X4), rhs_scale=hs[:], start=False, stop=True,
+                )
         for h in range(2):
             nc.scalar.copy(p_t[0][:, h * HO:(h + 1) * HO], pacc[h][0][:])
             nc.vector.tensor_copy(p_t[1][:, h * HO:(h + 1) * HO], pacc[h][1][:])

@@ -82,13 +82,12 @@ def tile_picked_codes_plain_one_chain_reminder_grouppairs_kernel(
         ta_t = [keep.tile([P, T], F32, name="ta%d" % t) for t in range(PACK)]
         nc.sync.dma_start(ta_t[0][:], ta_rows[0])
         l1 = load_list("l1", offs)
-        nc.sync.dma_start(ta_t[1][:], ta_rows[1])
         w_raw = keep.tile([P, 2 * R], U8, name="w_raw")
         nc.sync.dma_start(w_raw[:].bitcast(I32), w_words[0].bitcast(I32))
         w_stage = keep.tile([4, 4, R], U8, name="w_stage")
         nc.sync.dma_start(w_stage[:].bitcast(I32), w_scales[0].rearrange("(q r) n -> r q n", r=4).bitcast(I32))
-        nc.sync.dma_start(ta_t[2][:], ta_rows[2])
-        nc.sync.dma_start(ta_t[3][:], ta_rows[3])
+        for t in range(1, PACK):
+            nc.sync.dma_start(ta_t[t][:], ta_rows[t])
 
         w_plane = zeroed_plane("w_plane", R)
         xr_plane = zeroed_plane("xr_plane", V)
@@ -128,16 +127,16 @@ def tile_picked_codes_plain_one_chain_reminder_grouppairs_kernel(
         chunks = [(0, QJ), (QJ, QJ), (HJ, QJ), (HJ + QJ, EJ), (HJ + QJ + EJ, EJ)]
         on_scalar = [3, 4]
         xc4 = [keep.tile([P, n, PACK], BF16, name="xc4_%d" % c, align_bytes=ALIGN) for c, (j0, n) in enumerate(chunks)]
-        g01 = keep.tile([P, 2, J], BF16, name="g01")
         for t in range(2):
-            fetch(g01[:, t, :], ta_t[t], l1, 0, J, ga_t[:, t:t + 1])
-        for c, (j0, n) in enumerate(chunks):
-            nc.vector.tensor_copy(xc4[c][:, :, 0:2], g01[:, :, j0:j0 + n].rearrange("p e j -> p j e"))
+            g = keep.tile([P, J], BF16, name="g_whole%d" % t)
+            fetch(g[:], ta_t[t], l1, 0, J, ga_t[:, t:t + 1])
+            for c, (j0, n) in enumerate(chunks):
+                nc.vector.tensor_copy(xc4[c][:, :, t], g[:, j0:j0 + n])
         xq = [keep.tile([P, HJ], U32, name="xq%d" % h, align_bytes=ALIGN) for h in range(2)]
         xs = [keep.tile([P, HJ], U8, name="xs%d" % h, align_bytes=ALIGN) for h in range(2)]
         quantise_order = [[0, 1], [3, 2, 4]]
-        for t in range(2, PACK):
-            for h in range(2):
+        for t, halves in ((2, (1, 0)), (3, (0, 1))):
+            for h in halves:
                 tag = "g_upper" if h == 1 else "g_lower%d" % t
                 g = keep.tile([P, HJ], BF16, name="g", tag=tag)
                 fetch(g[:], ta_t[t], l1, h * HJ, HJ, ga_t[:, t:t + 1])

@@ -94,14 +94,14 @@ def tile_picked_codes_plain_one_chain_reminder_grouppairs_kernel(
         ws_plane = zeroed_plane("ws_plane", N)
         wb_plane = zeroed_plane("wb_plane", N)
 
-        l5 = load_list("l5", offs5)
-        xr_win = keep.tile([P, V], U16, name="xr_win")
-        nc.sync.dma_start(xr_win[:].bitcast(I32), xr_words[0].bitcast(I32))
-        load_scale_rows(xr_plane, xr_scales)
         l3 = load_list("l3", offs3)
         l4 = load_list("l4", offs4)
         sb_t = load_dealt("sb_t", sb, nc.sync)
         sd_t = load_dealt("sd_t", sd, nc.sync)
+        load_scale_rows(xr_plane, xr_scales)
+        l5 = load_list("l5", offs5)
+        xr_win = keep.tile([P, V], U16, name="xr_win")
+        nc.sync.dma_start(xr_win[:].bitcast(I32), xr_words[0].bitcast(I32))
         l2 = load_list("l2", offs2)
         sa_t = load_dealt("sa_t", sa, nc.sync)
         ws_w = load_e4m3_words("ws_w", ws_words)
@@ -124,8 +124,8 @@ def tile_picked_codes_plain_one_chain_reminder_grouppairs_kernel(
         nc.vector.tensor_copy(w_ds[:], w_plane[:].rearrange("p (m t) -> p t m", t=PACK))
 
         EJ = J // 8
-        chunks = [(0, QJ), (QJ, QJ), (HJ, QJ), (HJ + QJ, EJ), (HJ + QJ + EJ, EJ)]
-        on_scalar = [3, 4]
+        chunks = [(0, QJ), (QJ, QJ)] + [(HJ + i * EJ, EJ) for i in range(4)]
+        on_scalar = [3, 5]
         xc4 = [keep.tile([P, n, PACK], BF16, name="xc4_%d" % c, align_bytes=ALIGN) for c, (j0, n) in enumerate(chunks)]
         for t in range(2):
             g = keep.tile([P, J], BF16, name="g_whole%d" % t)
@@ -134,7 +134,7 @@ def tile_picked_codes_plain_one_chain_reminder_grouppairs_kernel(
                 nc.vector.tensor_copy(xc4[c][:, :, t], g[:, j0:j0 + n])
         xq = [keep.tile([P, HJ], U32, name="xq%d" % h, align_bytes=ALIGN) for h in range(2)]
         xs = [keep.tile([P, HJ], U8, name="xs%d" % h, align_bytes=ALIGN) for h in range(2)]
-        quantise_order = [[0, 1], [3, 2, 4]]
+        quantise_order = [[0, 1], [2, 3, 4, 5]]
         for t, halves in ((2, (1, 0)), (3, (0, 1))):
             for h in halves:
                 tag = "g_upper" if h == 1 else "g_lower%d" % t
@@ -157,8 +157,8 @@ def tile_picked_codes_plain_one_chain_reminder_grouppairs_kernel(
                         )
 
         a_t = [keep.tile([P, J], F32, name="a%d" % t) for t in range(PACK)]
-        pieces = [(0, 0, HJ, 0), (1, 0, HJ, 4), (0,) + chunks[3] + (1,), (0,) + chunks[2] + (2,), (0,) + chunks[4] + (3,),
-                  (1, HJ, HJ, 5), (2, HJ, HJ, 6), (2, 0, HJ, 3), (3, HJ, HJ, 7), (3, 0, HJ, 2)]
+        pieces = [(0, 0, HJ, 0), (1, 0, QJ, 5)] + [(0,) + chunks[c] + (c - 1,) for c in range(2, 6)] + [
+            (1, HJ, HJ, 6), (1, QJ, QJ, 3), (2, HJ, HJ, 7), (2, 0, HJ, 4), (3, HJ, HJ, 0), (3, 0, HJ, 2)]
         for i, (t, j0, n, bank) in enumerate(pieces):
             h, c0 = divmod(j0, HJ)
             acc = psum.tile([P, n], F32, name="acc", tag="bank%d" % bank)
@@ -166,7 +166,7 @@ def tile_picked_codes_plain_one_chain_reminder_grouppairs_kernel(
                 out=acc[:], lhsT=w_dw[:, t, :].bitcast(FP4X4), lhsT_scale=w_ds[:, t, :],
                 rhs=xq[h][:, c0:c0 + n].bitcast(FP8X4), rhs_scale=xs[h][:, c0:c0 + n], start=True, stop=True,
             )
-            if i in (0, 1, 4):
+            if i in (0, 1, 5):
                 nc.scalar.copy(a_t[t][:, j0:j0 + n], acc[:])
             else:
                 nc.vector.tensor_copy(a_t[t][:, j0:j0 + n], acc[:])
@@ -175,7 +175,7 @@ def tile_picked_codes_plain_one_chain_reminder_grouppairs_kernel(
         xr_gs = keep.tile([P, O], U8, name="xr_gs", tag="fp4_scales", align_bytes=ALIGN)
         nc.vector.tensor_copy(xr_gw[:], xr_win[:].indirect(l5[:]))
         nc.vector.tensor_copy(xr_gs[:], xr_plane[:].indirect(l5[:]))
-        p_banks = [[0, 1], [4, 5]]
+        p_banks = [[1, 5], [6, 7]]
         pacc = [[psum.tile([P, HO], F32, name="pacc", tag="bank%d" % p_banks[h][u]) for u in range(2)] for h in range(2)]
         for h in range(2):
             for u in range(2):

from contextlib import ExitStack

import concourse.mybir as mybir

K, J, R, T, O, S, N, Z, V, U = 512, 1024, 512, 2048, 256, 512, 256, 512, 1024, 128
FLOPS = 2 * (K * R * J + R * N * O + Z * N * O)

F32 = mybir.dt.float32
BF16 = mybir.dt.bfloat16
I32 = mybir.dt.int32
U32 = mybir.dt.uint32
U16 = mybir.dt.uint16
U8 = mybir.dt.uint8
FP8X4 = mybir.dt.float8_e4m3fn_x4
FP4X4 = mybir.dt.float4_e2m1fn_x4
ACT = mybir.ActivationFunctionType
ALU = mybir.AluOpType

P = 128
PACK = 4
STRIPE = 16
ALIGN = 64
HJ = J // 2
QJ = J // 4
HO = O // 2


def tile_picked_codes_plain_one_chain_reminder_grouppairs_kernel(
    tc, ta, ga, w_words, w_scales, sa, sb, sd, wb_words, wb_scales, xr_words, xr_scales,
    ws_words, ws_scales, so, sp, offs, offs2, offs3, offs4, offs5, offs6, offs7, out,
):
    nc = tc.nc

    with ExitStack() as ctx:
        lists = ctx.enter_context(tc.tile_pool(name="lists", bufs=1))
        keep = ctx.enter_context(tc.tile_pool(name="keep", bufs=1))
        psum = ctx.enter_context(tc.psum_pool(name="psum", bufs=1))

        def load_list(name, source):
            tile = lists.tile(list(source.shape), U16, name=name)
            nc.sync.dma_start(tile[:], source)
            return tile

        def load_dealt(name, source, queue):
            tile = keep.tile([P, PACK], F32, name=name)
            queue.dma_start(tile[:], source.rearrange("(p t) one -> p (t one)", t=PACK))
            return tile

        def load_blocks(name, source):
            tile = keep.tile([P, N // P], F32, name=name)
            with nc.allow_non_contiguous_dma(reason="one value a partition"):
                nc.sync.dma_start(tile[:], source.rearrange("(u p) one -> p (u one)", p=P))
            return tile

        def zeroed_plane(name, width):
            plane = keep.tile([P, width], U8, name=name, align_bytes=ALIGN)
            nc.vector.memset(plane[:].bitcast(I32), 0)
            return plane

        def load_scale_rows(plane, source):
            for q in range(4):
                nc.sync.dma_start(plane[32 * q:32 * q + 4, :].bitcast(I32), source[0, 4 * q:4 * q + 4, :].bitcast(I32))

        def load_e4m3_words(name, source):
            tile = keep.tile([P, N], U32, name=name, align_bytes=ALIGN)
            nc.sync.dma_start(tile[:].bitcast(I32), source[0].rearrange("p n t -> p (n t)").bitcast(I32))
            return tile

        def fetch(dst, window, lst, first, count, scale):
            nc.scalar.activation(
                out=dst, in_=window[:].indirect(lst[:, first // STRIPE:(first + count) // STRIPE]),
                func=ACT.Copy, scale=scale,
            )

        warm_in = keep.tile([P, 1], F32, name="warm_in")
        warm_out = keep.tile([P, 1], F32, name="warm_out")
        nc.gpsimd.memset(warm_in[:], 0.0)
        nc.scalar.activation(out=warm_out[:], in_=warm_in[:], func=ACT.Copy)

        ga_t = load_dealt("ga_t", ga, nc.scalar)
        ta_rows = ta.rearrange("(p t) c -> t p c", t=PACK)
        ta_t = [keep.tile([P, T], F32, name="ta%d" % t) for t in range(PACK)]
        nc.sync.dma_start(ta_t[0][:], ta_rows[0])
        l1 = load_list("l1", offs)
        w_raw = keep.tile([P, 2 * R], U8, name="w_raw")
        nc.sync.dma_start(w_raw[:].bitcast(I32), w_words[0].bitcast(I32))
        w_stage = keep.tile([4, 4, R], U8, name="w_stage")
        nc.sync.dma_start(w_stage[:].bitcast(I32), w_scales[0].rearrange("(q r) n -> r q n", r=4).bitcast(I32))
        for t in range(1, PACK):
            nc.sync.dma_start(ta_t[t][:], ta_rows[t])

        w_plane = zeroed_plane("w_plane", R)
        xr_plane = zeroed_plane("xr_plane", V)
        ws_plane = zeroed_plane("ws_plane", N)
        wb_plane = zeroed_plane("wb_plane", N)

        l3 = load_list("l3", offs3)
        l4 = load_list("l4", offs4)
        sb_t = load_dealt("sb_t", sb, nc.sync)
        sd_t = load_dealt("sd_t", sd, nc.sync)
        load_scale_rows(xr_plane, xr_scales)
        l5 = load_list("l5", offs5)
        xr_win = keep.tile([P, V], U16, name="xr_win")
        nc.sync.dma_start(xr_win[:].bitcast(I32), xr_words[0].bitcast(I32))
        l2 = load_list("l2", offs2)
        sa_t = load_dealt("sa_t", sa, nc.sync)
        ws_w = load_e4m3_words("ws_w", ws_words)
        load_scale_rows(ws_plane, ws_scales)
        wb_w = load_e4m3_words("wb_w", wb_words)
        load_scale_rows(wb_plane, wb_scales)
        l6 = load_list("l6", offs6)
        l7 = load_list("l7", offs7)
        so_t = load_blocks("so_t", so)
        sp_t = load_blocks("sp_t", sp)

        for q in range(4):
            nc.vector.tensor_copy(w_plane[32 * q:32 * q + 4, :].bitcast(I32), w_stage[:, q, :].bitcast(I32))
        w_dw = keep.tile([P, PACK, 2 * P], U8, name="w_dw", tag="fp4_words", align_bytes=ALIGN)
        w_ds = keep.tile([P, PACK, P], U8, name="w_ds", tag="fp4_scales", align_bytes=ALIGN)
        nc.vector.tensor_copy(
            w_dw[:].rearrange("p t (m b) -> p t m b", b=2),
            w_raw[:].rearrange("p (m t b) -> p t m b", t=PACK, b=2),
        )
        nc.vector.tensor_copy(w_ds[:], w_plane[:].rearrange("p (m t) -> p t m", t=PACK))

        EJ = J // 8
        chunks = [(0, QJ), (QJ, QJ)] + [(HJ + i * EJ, EJ) for i in range(4)]
        on_scalar = [3, 5]
        xc4 = [keep.tile([P, n, PACK], BF16, name="xc4_%d" % c, align_bytes=ALIGN) for c, (j0, n) in enumerate(chunks)]
        for t in range(2):
            g = keep.tile([P, J], BF16, name="g_whole%d" % t)
            fetch(g[:], ta_t[t], l1, 0, J, ga_t[:, t:t + 1])
            for c, (j0, n) in enumerate(chunks):
                nc.vector.tensor_copy(xc4[c][:, :, t], g[:, j0:j0 + n])
        xq = [keep.tile([P, HJ], U32, name="xq%d" % h, align_bytes=ALIGN) for h in range(2)]
        xs = [keep.tile([P, HJ], U8, name="xs%d" % h, align_bytes=ALIGN) for h in range(2)]
        quantise_order = [[0, 1], [2, 3, 4, 5]]
        for t, halves in ((2, (1, 0)), (3, (0, 1))):
            for h in halves:
                tag = "g_upper" if h == 1 else "g_lower%d" % t
                g = keep.tile([P, HJ], BF16, name="g", tag=tag)
                fetch(g[:], ta_t[t], l1, h * HJ, HJ, ga_t[:, t:t + 1])
                for c, (j0, n) in enumerate(chunks):
                    if j0 // HJ == h:
                        src = g[:, j0 - h * HJ:j0 - h * HJ + n]
                        if t == PACK - 1 and c in on_scalar:
                            nc.scalar.copy(xc4[c][:, :, t], src)
                        else:
                            nc.vector.tensor_copy(xc4[c][:, :, t], src)
                if t == PACK - 1:
                    for c in quantise_order[h]:
                        j0, n = chunks[c]
                        c0 = j0 - h * HJ
                        nc.vector.quantize_mx(
                            out=xq[h][:, c0:c0 + n].bitcast(FP8X4), scales=xs[h][:, c0:c0 + n],
                            in_=xc4[c][:].rearrange("p j t -> p (j t)"),
                        )

        a_t = [keep.tile([P, J], F32, name="a%d" % t) for t in range(PACK)]
        pieces = [(0, 0, HJ, 0), (1, 0, QJ, 5)] + [(0,) + chunks[c] + (c - 1,) for c in range(2, 6)] + [
            (1, HJ, HJ, 6), (1, QJ, QJ, 3), (2, HJ, HJ, 7), (2, 0, HJ, 4), (3, HJ, HJ, 0), (3, 0, HJ, 2)]
        for i, (t, j0, n, bank) in enumerate(pieces):
            h, c0 = divmod(j0, HJ)
            acc = psum.tile([P, n], F32, name="acc", tag="bank%d" % bank)
            nc.tensor.matmul_mx(
                out=acc[:], lhsT=w_dw[:, t, :].bitcast(FP4X4), lhsT_scale=w_ds[:, t, :],
                rhs=xq[h][:, c0:c0 + n].bitcast(FP8X4), rhs_scale=xs[h][:, c0:c0 + n], start=True, stop=True,
            )
            if i in (0, 1, 5):
                nc.scalar.copy(a_t[t][:, j0:j0 + n], acc[:])
            else:
                nc.vector.tensor_copy(a_t[t][:, j0:j0 + n], acc[:])

        xr_gw = keep.tile([P, O], U16, name="xr_gw", tag="fp4_words", align_bytes=ALIGN)
        xr_gs = keep.tile([P, O], U8, name="xr_gs", tag="fp4_scales", align_bytes=ALIGN)
        nc.vector.tensor_copy(xr_gw[:], xr_win[:].indirect(l5[:]))
        nc.vector.tensor_copy(xr_gs[:], xr_plane[:].indirect(l5[:]))
        p_banks = [[1, 5], [6, 7]]
        pacc = [[psum.tile([P, HO], F32, name="pacc", tag="bank%d" % p_banks[h][u]) for u in range(2)] for h in range(2)]
        for h in range(2):
            for u in range(2):
                nc.tensor.matmul_mx(
                    out=pacc[h][u][:], lhsT=ws_w[:, u * P:(u + 1) * P].bitcast(FP8X4), lhsT_scale=ws_plane[:, u * P:(u + 1) * P],
                    rhs=xr_gw[:, h * HO:(h + 1) * HO].bitcast(FP4X4), rhs_scale=xr_gs[:, h * HO:(h + 1) * HO],
                    start=True, stop=False,
                )

        hid4 = [keep.tile([P, HO, PACK], BF16, name="hid4_%d" % h, align_bytes=ALIGN) for h in range(2)]
        d01 = keep.tile([P, 2, O], BF16, name="d01")
        d23 = [keep.tile([P, 2, HO], BF16, name="d23_%d" % h) for h in range(2)]

        def magnitude(dst, src):
            view = src.rearrange("p e o -> p o e")
            nc.vector.scalar_tensor_tensor(dst, view, -1.0, view, ALU.mult, ALU.max)

        h1 = [keep.tile([P, S], F32, name="h1_%d" % t) for t in range(PACK)]

        def seats(t):
            fetch(h1[t][:], a_t[t], l2, 0, S, sa_t[:, t:t + 1])

        def difference(t, o0, n):
            own = keep.tile([P, n], F32, name="own_%d_%d" % (t, o0))
            shared = keep.tile([P, n], F32, name="shared_%d_%d" % (t, o0))
            fetch(own[:], h1[t], l3, o0, n, sb_t[:, t:t + 1])
            fetch(shared[:], h1[t], l4, o0, n, sd_t[:, t:t + 1])
            if t < 2:
                nc.vector.tensor_tensor(d01[:, t, :], own[:], shared[:], ALU.subtract)
            else:
                for h in range(o0 // HO, (o0 + n) // HO):
                    cols = slice(h * HO - o0, (h + 1) * HO - o0)
                    nc.vector.tensor_tensor(d23[h][:, t - 2, :], own[:, cols], shared[:, cols], ALU.subtract)
            return shared

        seats(0)
        for t in range(PACK - 1):
            seats(t + 1)
            difference(t, 0, O)
            if t == 1:
                for h in range(2):
                    magnitude(hid4[h][:, :, 0:2], d01[:, :, h * HO:(h + 1) * HO])
        for h in range(2):
            last = difference(PACK - 1, h * HO, HO)
        QO = HO // 2
        nc.scalar.activation(out=hid4[0][:, :, 2:4], in_=d23[0][:].rearrange("p e o -> p o e"), func=ACT.Abs)
        magnitude(hid4[1][:, :QO, 2:4], d23[1][:, :, :QO])
        nc.scalar.activation(out=hid4[1][:, QO:, 2:4], in_=d23[1][:, :, QO:].rearrange("p e o -> p o e"), func=ACT.Abs)

        p_t = [keep.tile([P, O], F32, name="p%d" % u) for u in range(2)]
        for h in range(2):
            hq = keep.tile([P, HO], U32, name="hq%d" % h, align_bytes=ALIGN)
            hs = keep.tile([P, HO], U8, name="hs%d" % h, align_bytes=ALIGN)
            nc.vector.quantize_mx(out=hq[:].bitcast(FP8X4), scales=hs[:], in_=hid4[h][:].rearrange("p o t -> p (o t)"))
            for u in range(2):
                nc.tensor.matmul_mx(
                    out=pacc[h][u][:], lhsT=wb_w[:, u * P:(u + 1) * P].bitcast(FP8X4), lhsT_scale=wb_plane[:, u * P:(u + 1) * P],
                    rhs=hq[:].bitcast(FP8X4), rhs_scale=hs[:], start=False, stop=True,
                )
        for h in range(2):
            nc.scalar.copy(p_t[0][:, h * HO:(h + 1) * HO], pacc[h][0][:])
            nc.vector.tensor_copy(p_t[1][:, h * HO:(h + 1) * HO], pacc[h][1][:])

        for u in range(2):
            first = keep.tile([P, U], F32, name="first%d" % u)
            second = keep.tile([P, U], F32, name="second%d" % u)
            larger = keep.tile([P, U], F32, name="larger%d" % u)
            fetch(first[:], p_t[u], l6, 0, U, so_t[:, u:u + 1])
            fetch(second[:], p_t[u], l7, 0, U, sp_t[:, u:u + 1])
            nc.vector.tensor_tensor(larger[:], first[:], second[:], ALU.max)
            nc.sync.dma_start(out[u * P:(u + 1) * P, :], larger[:])
